import numpy as np
import ml_dtypes


def mxq(x, axis, fmt="e4m3"):
    dtype, down = {"e4m3": (ml_dtypes.float8_e4m3fn, 7), "e5m2": (ml_dtypes.float8_e5m2, 14)}[fmt]
    v = np.moveaxis(np.asarray(x, np.float32).astype(ml_dtypes.bfloat16).astype(np.float64), axis, -1)
    blocks = v.reshape(v.shape[:-1] + (-1, 32))
    amax = np.abs(blocks).max(-1, keepdims=True)
    byte = np.maximum(np.where(amax > 0, np.frexp(amax)[1] - 1 + 127, 0) - down, 1)
    scale = np.exp2(byte - 127.0)
    codes = (blocks / scale).astype(np.float32).astype(dtype).astype(np.float64)
    return np.moveaxis((codes * scale).reshape(v.shape), -1, axis)


WIDE = False


def mx_kscale(k):
    if not WIDE:
        return np.ones(k)
    levels = np.array([10, -10, 5, -5, 0])
    if k % 512:
        return np.exp2(np.random.permutation(np.resize(levels, k // 32))).repeat(32)
    a = np.empty((k // 512, 16))
    for p in range(k // 512):
        a[p, :8] = np.random.permutation(np.resize(levels, 8))
        for g in range(8):
            far = levels[np.abs(levels - a[p, g]) >= 10]
            a[p, g + 8] = far[np.random.randint(len(far))]
    return np.exp2(a.ravel()).repeat(32)


def f64(x):
    return np.asarray(x).astype(np.float64)


def striped(idx):
    return np.tile(idx.reshape(-1, 16).T, (8, 1)).astype(np.uint16)


def unstriped(offs):
    return offs[:16].T.reshape(-1).astype(np.int64)


E2M1 = np.array([0.0, 0.5, 1.0, 1.5, 2.0, 3.0, 4.0, 6.0, -0.0, -0.5, -1.0, -1.5, -2.0, -3.0, -4.0, -6.0])


def pack_fp4(w):
    k, n = w.shape
    w = f64(np.asarray(w, np.float32).astype(ml_dtypes.bfloat16)).reshape(k // 32, 32, n)
    amax = np.abs(w).max(1)
    mant, ex = np.frexp(amax / 6.0)
    byte = np.clip(np.where(amax > 0, np.where(mant > 0.5, ex, ex - 1) + 127, 1), 1, 254)
    scaled = (w * np.exp2(127.0 - byte)[:, None, :]).reshape(k, n).astype(np.float32)
    c = np.ascontiguousarray(scaled.reshape(k // 512, 128, 4, n).transpose(0, 1, 3, 2)).astype(ml_dtypes.float4_e2m1fn).view(np.uint8) & 0xF
    words = (c[..., 0::2] | (c[..., 1::2] << 4)).reshape(k // 512, 128, 2 * n)
    return np.ascontiguousarray(words), np.ascontiguousarray(byte.astype(np.uint8).reshape(k // 512, 16, n))


def unpack_fp4(words, scales):
    g, _, n = scales.shape
    words = np.ascontiguousarray(words).reshape(g, 128, n, 2)
    nib = np.empty((g, 128, n, 4), np.uint8)
    nib[..., 0::2] = words & 0xF
    nib[..., 1::2] = words >> 4
    vals = E2M1[nib] * np.repeat(np.exp2(scales.astype(np.float64) - 127.0), 8, axis=1)[..., None]
    return vals.transpose(0, 1, 3, 2).reshape(g * 512, n)


def gelu(v):
    return 0.5 * v * (1.0 + np.tanh(np.sqrt(2.0 / np.pi) * (v + 0.044715 * v**3)))


K, T, S, V, H, N = 512, 1024, 512, 256, 512, 256


def setup_inputs():
    n = np.random.standard_normal
    s = mx_kscale(K)[:, None]
    u = mx_kscale(H)
    packed_w3 = pack_fp4(n((H, N)) / np.sqrt(H) / u[:, None])
    return {
        "xT": (n((K, T)) * s).astype(np.float32),
        "w1": (n((K, H)) / np.sqrt(2 * K) / s * u).astype(np.float32),
        "w2": (n((K, H)) / np.sqrt(2 * K) / s * u).astype(np.float32),
        "w3_words": packed_w3[0],
        "w3_scales": packed_w3[1],
        "offs": striped(np.random.permutation(T)[:S]),
        "cen": striped(np.random.permutation(S)[:V]),
        "pos1": striped(np.random.permutation(S)[:V]),
        "pos2": striped(np.random.permutation(S)[:V]),
        "pos3": striped(np.random.permutation(S)[:V]),
        "pos4": striped(np.random.permutation(S)[:V]),
    }


def reference(xT, w1, w2, w3_words, w3_scales, offs, cen, pos1, pos2, pos3, pos4):
    xq = mxq(f64(xT)[:, unstriped(offs)], 0, "e4m3")
    y = mxq(f64(w1), 0, "e4m3").T @ xq
    yc = y[:, unstriped(cen)]
    e = mxq(f64(w2), 0, "e4m3").T @ xq
    z = np.maximum(np.maximum(np.maximum(gelu(yc + e[:, unstriped(pos1)]), gelu(yc + e[:, unstriped(pos2)])), gelu(yc + e[:, unstriped(pos3)])), gelu(yc + e[:, unstriped(pos4)]))
    return unpack_fp4(w3_words, w3_scales).T @ mxq(z, 0, "e4m3")

@@ -1,0 +1,171 @@
+from contextlib import ExitStack
+
+import concourse.mybir as mybir
+
+K, T, S, V, H, N = 512, 1024, 512, 256, 512, 256
+FLOPS = 2 * (2 * K * H * S + H * N * V)
+
+F32 = mybir.dt.float32
+BF16 = mybir.dt.bfloat16
+U32 = mybir.dt.uint32
+I32 = mybir.dt.int32
+U16 = mybir.dt.uint16
+U8 = mybir.dt.uint8
+FP8X4 = mybir.dt.float8_e4m3fn_x4
+FP4X4 = mybir.dt.float4_e2m1fn_x4
+ADD = mybir.AluOpType.add
+MAX = mybir.AluOpType.max
+GELU = mybir.ActivationFunctionType.Gelu_apprx_tanh
+
+P = 128
+PACK = 4
+HALF = V // 2
+
+
+def tile_picked_edgecv_gelu_e_kernel(
+    tc, xT, w1, w2, w3_words, w3_scales, offs, cen, pos1, pos2, pos3, pos4, out
+):
+    nc = tc.nc
+    with ExitStack() as ctx:
+        lists = ctx.enter_context(tc.tile_pool(name="lists", bufs=1))
+        keep = ctx.enter_context(tc.tile_pool(name="keep", bufs=1))
+        psum = ctx.enter_context(tc.psum_pool(name="psum", bufs=1))
+
+        def sb(name, shape, dtype):
+            return keep.tile(shape, dtype, name=name, align_bytes=64)
+
+        warm_in = sb("warm_in", [P, 1], F32)
+        warm_out = sb("warm_out", [P, 1], F32)
+        nc.vector.memset(warm_in[:], 0.0)
+        nc.scalar.activation(warm_out[:], warm_in[:], GELU)
+        w3_scale = sb("w3_scale", [P, N], U8)
+        nc.gpsimd.memset(w3_scale[:], 0)
+
+        x_rows = xT.rearrange("(p j) n -> p j n", j=PACK)
+        x_plane = [sb(f"x_plane{j}", [P, T], F32) for j in range(PACK)]
+        offs_sb = lists.tile([P, S // 16], U16, name="offs_sb")
+        nc.sync.dma_start(x_plane[0][:], x_rows[:, 0, :])
+        nc.sync.dma_start(offs_sb[:], offs)
+        for j in range(1, PACK):
+            nc.sync.dma_start(x_plane[j][:], x_rows[:, j, :])
+        w_raw = {}
+        for name, w in (("w1", w1), ("w2", w2)):
+            w_rows = w.rearrange("(p j) c -> p j c", j=PACK)
+            for h in range(2):
+                w_raw[name, h] = sb(f"{name}_raw{h}", [P, PACK, H // 2], F32)
+                nc.sync.dma_start(w_raw[name, h][:], w_rows[:, :, h * (H // 2) : (h + 1) * (H // 2)])
+        cen_sb = lists.tile([P, V // 16], U16, name="cen_sb")
+        nc.sync.dma_start(cen_sb[:], cen)
+        pos_sb = []
+        for d, pos in enumerate((pos1, pos2, pos3, pos4)):
+            pos_sb.append(lists.tile([P, V // 16], U16, name=f"pos_sb{d}"))
+            nc.sync.dma_start(pos_sb[d][:], pos)
+        w3_code = sb("w3_code", [P, 2 * N], U8)
+        nc.sync.dma_start(w3_code[:], w3_words[0])
+        for q in range(4):
+            nc.sync.dma_start(
+                w3_scale[32 * q : 32 * q + 4, :].bitcast(I32), w3_scales[0, 4 * q : 4 * q + 4, :].bitcast(I32)
+            )
+
+        picked = [sb(f"picked{u}", [P, 2, S], F32) for u in range(2)]
+        x_bf = sb("x_bf", [P, S, PACK], BF16)
+        for j in range(PACK):
+            nc.vector.tensor_copy(picked[j // 2][:, j % 2, :], x_plane[j][:].indirect(offs_sb[:]))
+            if j == 1:
+                nc.scalar.copy(x_bf[:, :, 0:2], picked[0][:].rearrange("p j n -> p n j"))
+        nc.vector.tensor_copy(x_bf[:, :, 2:4], picked[1][:].rearrange("p j n -> p n j"))
+
+        w_bf = {name: sb(f"{name}_bf", [P, PACK, P, PACK], BF16) for name in ("w1", "w2")}
+
+        def deal(engine, name, h, m0, m1):
+            src = w_raw[name, h][:].rearrange("p j (m t) -> p m j t", t=PACK)[:, m0 - 64 * h : m1 - 64 * h]
+            dst = w_bf[name][:].rearrange("p t m j -> p m j t")[:, m0:m1]
+            if engine == "scalar":
+                nc.scalar.copy(dst, src)
+            else:
+                nc.vector.tensor_copy(dst, src)
+
+        deal("scalar", "w1", 0, 0, 64)
+        deal("scalar", "w1", 1, 64, 96)
+        deal("vector", "w1", 1, 96, 128)
+
+        x_code = sb("x_code", [P, S], U32)
+        x_scale = sb("x_scale", [P, S], U8)
+        nc.vector.quantize_mx(x_code[:].bitcast(FP8X4), x_scale[:], x_bf[:].rearrange("p n j -> p (n j)"))
+
+        def quantise_w(name):
+            code = sb(f"{name}_code", [P, H], U32)
+            scale = sb(f"{name}_scale", [P, H], U8)
+            nc.vector.quantize_mx(code[:].bitcast(FP8X4), scale[:], w_bf[name][:].rearrange("p t m j -> p (t m j)"))
+            return code, scale
+
+        def product(name, code, scale):
+            rows = []
+            for t in range(PACK):
+                acc = psum.tile([P, S], F32, name=f"acc{t}", tag=f"acc{t}")
+                cols = slice(t * P, (t + 1) * P)
+                nc.tensor.matmul_mx(
+                    acc[:], code[:, cols].bitcast(FP8X4), scale[:, cols], x_code[:].bitcast(FP8X4), x_scale[:],
+                    start=True, stop=True,
+                )
+                row = sb(f"{name}_row{t}", [P, S], F32)
+                nc.scalar.copy(row[:], acc[:])
+                rows.append(row)
+            return rows
+
+        w1_code, w1_scale = quantise_w("w1")
+        y = product("y", w1_code, w1_scale)
+        deal("vector", "w2", 0, 0, 64)
+        deal("vector", "w2", 1, 64, 128)
+        w2_code, w2_scale = quantise_w("w2")
+        e = product("e", w2_code, w2_scale)
+
+        yc = sb("yc", [P, PACK, V], F32)
+        for t in range(PACK):
+            nc.vector.tensor_copy(yc[:, t, :], y[t][:].indirect(cen_sb[:]))
+
+        def edges(d, v0, v1):
+            width = v1 - v0
+            u = sb(f"u{d}_{v0}", [P, PACK, width], F32)
+            for t in range(PACK):
+                nc.vector.tensor_tensor(
+                    u[:, t, :], e[t][:].indirect(pos_sb[d][:, v0 // 16 : v1 // 16]), yc[:, t, v0:v1], ADD
+                )
+            g = sb(f"g{d}_{v0}", [P, width * PACK], BF16)
+            nc.scalar.activation(
+                g[:].rearrange("p (c i t) -> p c t i", i=4, t=PACK),
+                u[:].rearrange("p t (c i) -> p c t i", i=4),
+                GELU,
+            )
+            return g
+
+        g0 = edges(0, 0, V)
+        g1 = edges(1, 0, V)
+        g2 = edges(2, 0, V)
+        m01 = sb("m01", [P, V * PACK], BF16)
+        nc.vector.tensor_tensor(m01[:], g0[:], g1[:], MAX)
+        g3 = [edges(3, 0, HALF)]
+        m012 = sb("m012", [P, V * PACK], BF16)
+        nc.vector.tensor_tensor(m012[:], m01[:], g2[:], MAX)
+        g3.append(edges(3, HALF, V))
+
+        out_rows = out.rearrange("(b p) v -> p b v", p=P)
+        for h in range(2):
+            z = sb(f"z{h}", [P, HALF * PACK], BF16)
+            nc.vector.tensor_tensor(z[:], m012[:, h * HALF * PACK : (h + 1) * HALF * PACK], g3[h][:], MAX)
+            z_code = sb(f"z_code{h}", [P, HALF], U32)
+            z_scale = sb(f"z_scale{h}", [P, HALF], U8)
+            nc.vector.quantize_mx(z_code[:].bitcast(FP8X4), z_scale[:], z[:])
+            acc = psum.tile([P, 2, HALF], F32, name=f"out_acc{h}")
+            for b in range(2):
+                nc.tensor.matmul_mx(
+                    acc[:, b, :],
+                    w3_code[:, 2 * P * b : 2 * P * (b + 1)].bitcast(FP4X4),
+                    w3_scale[:, P * b : P * (b + 1)],
+                    z_code[:].bitcast(FP8X4),
+                    z_scale[:],
+                    start=True, stop=True,
+                )
+            res = sb(f"res{h}", [P, 2, HALF], F32)
+            nc.scalar.copy(res[:], acc[:])
+            nc.sync.dma_start(out_rows[:, :, h * HALF : (h + 1) * HALF], res[:])

@@ -31,29 +31,51 @@ def tile_picked_edgecv_gelu_e_kernel(
         keep = ctx.enter_context(tc.tile_pool(name="keep", bufs=1))
         psum = ctx.enter_context(tc.psum_pool(name="psum", bufs=1))
 
-        def sb(name, shape, dtype):
-            return keep.tile(shape, dtype, name=name, align_bytes=64)
+        def sb(name, shape, dtype, tag=None):
+            return keep.tile(shape, dtype, name=name, tag=tag or name, align_bytes=64)
+
+        def bank(name, shape, b):
+            return psum.tile(shape, F32, name=name, tag=f"bank{b}")
 
         warm_in = sb("warm_in", [P, 1], F32)
         warm_out = sb("warm_out", [P, 1], F32)
         nc.vector.memset(warm_in[:], 0.0)
         nc.scalar.activation(warm_out[:], warm_in[:], GELU)
         w3_scale = sb("w3_scale", [P, N], U8)
-        nc.gpsimd.memset(w3_scale[:], 0)
+        nc.vector.memset(w3_scale[:].bitcast(I32), 0)
 
         x_rows = xT.rearrange("(p j) n -> p j n", j=PACK)
-        x_plane = [sb(f"x_plane{j}", [P, T], F32) for j in range(PACK)]
         offs_sb = lists.tile([P, S // 16], U16, name="offs_sb")
-        nc.sync.dma_start(x_plane[0][:], x_rows[:, 0, :])
-        nc.sync.dma_start(offs_sb[:], offs)
-        for j in range(1, PACK):
-            nc.sync.dma_start(x_plane[j][:], x_rows[:, j, :])
+        x_pair = [sb(f"x_pair{u}", [P, T], U32) for u in range(2)]
+        x_raw = []
+        pieces = [(0, 0, 512), (0, 512, 1024), (1, 0, 512), (1, 512, 896), (1, 896, 1024)]
+        for n, (u, c0, c1) in enumerate(pieces):
+            x_raw.append(sb(f"x_raw{n}", [P, 2, c1 - c0], F32))
+            nc.sync.dma_start(x_raw[n][:], x_rows[:, 2 * u : 2 * u + 2, c0:c1])
+            if n == 0:
+                nc.sync.dma_start(offs_sb[:], offs)
+
+        def pair_up(copy, n, c0, c1):
+            u, first = pieces[n][:2]
+            copy(
+                x_pair[u][:, c0:c1].bitcast(BF16).rearrange("p (n s) -> p n s", s=2),
+                x_raw[n][:, :, c0 - first : c1 - first].rearrange("p s n -> p n s"),
+            )
+
+        pair_up(nc.vector.tensor_copy, 0, 0, 512)
+        pair_up(nc.vector.tensor_copy, 1, 512, 864)
+        pair_up(nc.scalar.copy, 1, 864, 1024)
+        pair_up(nc.scalar.copy, 2, 0, 512)
+        pair_up(nc.vector.tensor_copy, 3, 512, 896)
+        pair_up(nc.scalar.copy, 4, 896, 1024)
         w_raw = {}
+        cuts = {"w1": (0, 96, 128), "w2": (0, 96, 128)}
         for name, w in (("w1", w1), ("w2", w2)):
             w_rows = w.rearrange("(p j) c -> p j c", j=PACK)
             for h in range(2):
-                w_raw[name, h] = sb(f"{name}_raw{h}", [P, PACK, H // 2], F32)
-                nc.sync.dma_start(w_raw[name, h][:], w_rows[:, :, h * (H // 2) : (h + 1) * (H // 2)])
+                c0, c1 = PACK * cuts[name][h], PACK * cuts[name][h + 1]
+                w_raw[name, h] = sb(f"{name}_raw{h}", [P, PACK, c1 - c0], F32)
+                nc.sync.dma_start(w_raw[name, h][:], w_rows[:, :, c0:c1])
         cen_sb = lists.tile([P, V // 16], U16, name="cen_sb")
         nc.sync.dma_start(cen_sb[:], cen)
         pos_sb = []
@@ -67,105 +89,124 @@ def tile_picked_edgecv_gelu_e_kernel(
                 w3_scale[32 * q : 32 * q + 4, :].bitcast(I32), w3_scales[0, 4 * q : 4 * q + 4, :].bitcast(I32)
             )
 
-        picked = [sb(f"picked{u}", [P, 2, S], F32) for u in range(2)]
-        x_bf = sb("x_bf", [P, S, PACK], BF16)
-        for j in range(PACK):
-            nc.vector.tensor_copy(picked[j // 2][:, j % 2, :], x_plane[j][:].indirect(offs_sb[:]))
-            if j == 1:
-                nc.scalar.copy(x_bf[:, :, 0:2], picked[0][:].rearrange("p j n -> p n j"))
-        nc.vector.tensor_copy(x_bf[:, :, 2:4], picked[1][:].rearrange("p j n -> p n j"))
-
-        w_bf = {name: sb(f"{name}_bf", [P, PACK, P, PACK], BF16) for name in ("w1", "w2")}
-
-        def deal(engine, name, h, m0, m1):
-            src = w_raw[name, h][:].rearrange("p j (m t) -> p m j t", t=PACK)[:, m0 - 64 * h : m1 - 64 * h]
-            dst = w_bf[name][:].rearrange("p t m j -> p m j t")[:, m0:m1]
-            if engine == "scalar":
-                nc.scalar.copy(dst, src)
-            else:
-                nc.vector.tensor_copy(dst, src)
-
-        deal("scalar", "w1", 0, 0, 64)
-        deal("scalar", "w1", 1, 64, 96)
-        deal("vector", "w1", 1, 96, 128)
-
+        picked = [sb(f"picked{a}", [P, 2, S // 2], U32) for a in range(2)]
+        for u in range(2):
+            for a in range(2):
+                nc.vector.tensor_copy(picked[a][:, u, :], x_pair[u][:].indirect(offs_sb[:, 16 * a : 16 * a + 16]))
+        x_bf = [sb(f"x_bf{a}", [P, S], I32) for a in range(2)]
+        for a in range(2):
+            nc.vector.tensor_copy(
+                x_bf[a][:].rearrange("p (n u) -> p n u", u=2), picked[a][:].bitcast(I32).rearrange("p u n -> p n u")
+            )
         x_code = sb("x_code", [P, S], U32)
         x_scale = sb("x_scale", [P, S], U8)
-        nc.vector.quantize_mx(x_code[:].bitcast(FP8X4), x_scale[:], x_bf[:].rearrange("p n j -> p (n j)"))
+        for a in range(2):
+            cols = slice(a * S // 2, (a + 1) * S // 2)
+            nc.vector.quantize_mx(x_code[:, cols].bitcast(FP8X4), x_scale[:, cols], x_bf[a][:].bitcast(BF16))
 
-        def quantise_w(name):
-            code = sb(f"{name}_code", [P, H], U32)
-            scale = sb(f"{name}_scale", [P, H], U8)
-            nc.vector.quantize_mx(code[:].bitcast(FP8X4), scale[:], w_bf[name][:].rearrange("p t m j -> p (t m j)"))
+        w_bf = {key: sb(f"{key[0]}_bf{key[1]}", [P, 2, P, PACK], BF16) for key in (("w1", 0), ("w1", 1), ("w2", 0))}
+
+        def deal(copy, name, h, u):
+            src = w_raw[name, h][:].rearrange("p j (m t) -> p m j t", t=PACK)[:, :, :, 2 * u : 2 * u + 2]
+            dst = w_bf[name, u][:].rearrange("p t m j -> p m j t")[:, cuts[name][h] : cuts[name][h + 1]]
+            copy(dst, src)
+
+        def quantise_w(name, u):
+            code = sb(f"{name}_code{u}", [P, H // 2], U32)
+            scale = sb(f"{name}_scale{u}", [P, H // 2], U8)
+            nc.vector.quantize_mx(code[:].bitcast(FP8X4), scale[:], w_bf[name, u][:].rearrange("p t m j -> p (t m j)"))
             return code, scale
 
-        def product(name, code, scale):
-            rows = []
-            for t in range(PACK):
-                acc = psum.tile([P, S], F32, name=f"acc{t}", tag=f"acc{t}")
-                cols = slice(t * P, (t + 1) * P)
+        def product(name, t, parts, banks):
+            code, scale = parts
+            cols = slice((t % 2) * P, (t % 2 + 1) * P)
+            row = sb(f"{name}_row{t}", [P, S], F32)
+            width = S // len(banks)
+            for n, b in enumerate(banks):
+                acc = bank(f"{name}_acc{t}_{n}", [P, width], b)
+                span = slice(n * width, (n + 1) * width)
                 nc.tensor.matmul_mx(
-                    acc[:], code[:, cols].bitcast(FP8X4), scale[:, cols], x_code[:].bitcast(FP8X4), x_scale[:],
-                    start=True, stop=True,
+                    acc[:], code[:, cols].bitcast(FP8X4), scale[:, cols],
+                    x_code[:, span].bitcast(FP8X4), x_scale[:, span], start=True, stop=True,
                 )
-                row = sb(f"{name}_row{t}", [P, S], F32)
-                nc.scalar.copy(row[:], acc[:])
-                rows.append(row)
-            return rows
+                nc.scalar.copy(row[:, span], acc[:])
+            return row
 
-        w1_code, w1_scale = quantise_w("w1")
-        y = product("y", w1_code, w1_scale)
-        deal("vector", "w2", 0, 0, 64)
-        deal("vector", "w2", 1, 64, 128)
-        w2_code, w2_scale = quantise_w("w2")
-        e = product("e", w2_code, w2_scale)
+        deal(nc.scalar.copy, "w1", 0, 0)
+        deal(nc.scalar.copy, "w1", 1, 0)
+        deal(nc.scalar.copy, "w1", 0, 1)
+        w1_lo = quantise_w("w1", 0)
+        deal(nc.vector.tensor_copy, "w2", 0, 0)
+        y = [product("y", t, w1_lo, [t]) for t in (0, 1)]
+        deal(nc.vector.tensor_copy, "w1", 1, 1)
+        deal(nc.vector.tensor_copy, "w2", 1, 0)
+        w1_hi = quantise_w("w1", 1)
+        w2_lo = quantise_w("w2", 0)
+        e = [product("e", 0, w2_lo, [4, 2]), product("e", 1, w2_lo, [3])]
+        w_bf["w2", 1] = sb("w2_bf1", [P, 2, P, PACK], BF16, "w2_code0")
+        deal(nc.scalar.copy, "w2", 0, 1)
+        deal(nc.scalar.copy, "w2", 1, 1)
+        w2_hi = quantise_w("w2", 1)
+        y.extend(product("y", t, w1_hi, [t]) for t in (2, 3))
+        e.extend(product("e", t, w2_hi, [t - 2]) for t in (2, 3))
 
-        yc = sb("yc", [P, PACK, V], F32)
+        yc = sb("yc", [P, PACK, V], F32, "w2_bf0")
         for t in range(PACK):
             nc.vector.tensor_copy(yc[:, t, :], y[t][:].indirect(cen_sb[:]))
 
-        def edges(d, v0, v1):
-            width = v1 - v0
-            u = sb(f"u{d}_{v0}", [P, PACK, width], F32)
-            for t in range(PACK):
-                nc.vector.tensor_tensor(
-                    u[:, t, :], e[t][:].indirect(pos_sb[d][:, v0 // 16 : v1 // 16]), yc[:, t, v0:v1], ADD
-                )
-            g = sb(f"g{d}_{v0}", [P, width * PACK], BF16)
-            nc.scalar.activation(
-                g[:].rearrange("p (c i t) -> p c t i", i=4, t=PACK),
-                u[:].rearrange("p t (c i) -> p c t i", i=4),
-                GELU,
-            )
-            return g
+        g = [sb(f"g{d}", [P, 2, V, 2], BF16) for d in range(4)]
+        for u in range(2):
+            sums = [sb(f"sum{d}_{u}", [P, 2, V], F32, "w2_code0" if (d, u) == (3, 0) else None) for d in range(4)]
+            for s in range(2):
+                t = 2 * u + s
+                for d in range(4):
+                    nc.vector.tensor_tensor(sums[d][:, s, :], e[t][:].indirect(pos_sb[d][:]), yc[:, t, :], ADD)
+                    if s == 1:
+                        nc.scalar.activation(g[d][:, u], sums[d][:].rearrange("p s v -> p v s"), GELU)
 
-        g0 = edges(0, 0, V)
-        g1 = edges(1, 0, V)
-        g2 = edges(2, 0, V)
-        m01 = sb("m01", [P, V * PACK], BF16)
-        nc.vector.tensor_tensor(m01[:], g0[:], g1[:], MAX)
-        g3 = [edges(3, 0, HALF)]
-        m012 = sb("m012", [P, V * PACK], BF16)
-        nc.vector.tensor_tensor(m012[:], m01[:], g2[:], MAX)
-        g3.append(edges(3, HALF, V))
+        def larger(name, h, left, right):
+            m = sb(f"{name}_{h}", [P, 2, HALF, 2], BF16)
+            nc.vector.tensor_tensor(m[:], left, right[:, :, h * HALF : (h + 1) * HALF, :], MAX)
+            return m
+
+        m01 = [larger("m01", h, g[0][:, :, h * HALF : (h + 1) * HALF, :], g[1]) for h in range(2)]
+        m012 = [larger("m012", h, m01[h][:], g[2]) for h in range(2)]
+
+        def fourth(h):
+            z = sb(f"z{h}", [P, HALF * PACK], BF16)
+            cols = slice(h * HALF, (h + 1) * HALF)
+            nc.vector.tensor_tensor(
+                z[:].rearrange("p (v u s) -> p v u s", u=2, s=2),
+                m012[h][:].rearrange("p u v s -> p v u s"),
+                g[3][:, :, cols, :].rearrange("p u v s -> p v u s"),
+                MAX,
+            )
+            return z
 
         out_rows = out.rearrange("(b p) v -> p b v", p=P)
-        for h in range(2):
-            z = sb(f"z{h}", [P, HALF * PACK], BF16)
-            nc.vector.tensor_tensor(z[:], m012[:, h * HALF * PACK : (h + 1) * HALF * PACK], g3[h][:], MAX)
+
+        def project(h, z):
             z_code = sb(f"z_code{h}", [P, HALF], U32)
             z_scale = sb(f"z_scale{h}", [P, HALF], U8)
             nc.vector.quantize_mx(z_code[:].bitcast(FP8X4), z_scale[:], z[:])
-            acc = psum.tile([P, 2, HALF], F32, name=f"out_acc{h}")
             for b in range(2):
+                acc = bank(f"out_acc{h}_{b}", [P, HALF], 4 + 2 * h + b)
                 nc.tensor.matmul_mx(
-                    acc[:, b, :],
+                    acc[:],
                     w3_code[:, 2 * P * b : 2 * P * (b + 1)].bitcast(FP4X4),
                     w3_scale[:, P * b : P * (b + 1)],
                     z_code[:].bitcast(FP8X4),
                     z_scale[:],
                     start=True, stop=True,
                 )
-            res = sb(f"res{h}", [P, 2, HALF], F32)
-            nc.scalar.copy(res[:], acc[:])
-            nc.sync.dma_start(out_rows[:, :, h * HALF : (h + 1) * HALF], res[:])
+                res = sb(f"res{h}_{b}", [P, HALF], F32)
+                if h == 1 and b == 1:
+                    nc.vector.tensor_copy(res[:], acc[:])
+                else:
+                    nc.scalar.copy(res[:], acc[:])
+                nc.sync.dma_start(out_rows[:, b, h * HALF : (h + 1) * HALF], res[:])
+
+        z0 = fourth(0)
+        z1 = fourth(1)
+        project(0, z0)
+        project(1, z1)

@@ -48,7 +48,7 @@ def tile_picked_edgecv_gelu_e_kernel(
         offs_sb = lists.tile([P, S // 16], U16, name="offs_sb")
         x_pair = [sb(f"x_pair{u}", [P, T], U32) for u in range(2)]
         x_raw = []
-        pieces = [(0, 0, 512), (0, 512, 1024), (1, 0, 512), (1, 512, 896), (1, 896, 1024)]
+        pieces = [(0, 0, 1024), (1, 0, 512), (1, 512, 1024)]
         for n, (u, c0, c1) in enumerate(pieces):
             x_raw.append(sb(f"x_raw{n}", [P, 2, c1 - c0], F32))
             nc.sync.dma_start(x_raw[n][:], x_rows[:, 2 * u : 2 * u + 2, c0:c1])
@@ -62,20 +62,15 @@ def tile_picked_edgecv_gelu_e_kernel(
                 x_raw[n][:, :, c0 - first : c1 - first].rearrange("p s n -> p n s"),
             )
 
-        pair_up(nc.vector.tensor_copy, 0, 0, 512)
-        pair_up(nc.vector.tensor_copy, 1, 512, 864)
-        pair_up(nc.scalar.copy, 1, 864, 1024)
-        pair_up(nc.scalar.copy, 2, 0, 512)
-        pair_up(nc.vector.tensor_copy, 3, 512, 896)
-        pair_up(nc.scalar.copy, 4, 896, 1024)
+        pair_up(nc.vector.tensor_copy, 0, 0, 672)
+        pair_up(nc.scalar.copy, 0, 672, 1024)
+        pair_up(nc.scalar.copy, 1, 0, 512)
+        pair_up(nc.vector.tensor_copy, 2, 512, 848)
+        pair_up(nc.scalar.copy, 2, 848, 1024)
         w_raw = {}
-        cuts = {"w1": (0, 96, 128), "w2": (0, 96, 128)}
         for name, w in (("w1", w1), ("w2", w2)):
-            w_rows = w.rearrange("(p j) c -> p j c", j=PACK)
-            for h in range(2):
-                c0, c1 = PACK * cuts[name][h], PACK * cuts[name][h + 1]
-                w_raw[name, h] = sb(f"{name}_raw{h}", [P, PACK, c1 - c0], F32)
-                nc.sync.dma_start(w_raw[name, h][:], w_rows[:, :, c0:c1])
+            w_raw[name] = sb(f"{name}_raw", [P, PACK, H], F32)
+            nc.sync.dma_start(w_raw[name][:], w.rearrange("(p j) c -> p j c", j=PACK))
         cen_sb = lists.tile([P, V // 16], U16, name="cen_sb")
         nc.sync.dma_start(cen_sb[:], cen)
         pos_sb = []
@@ -94,22 +89,24 @@ def tile_picked_edgecv_gelu_e_kernel(
             for a in range(2):
                 nc.vector.tensor_copy(picked[a][:, u, :], x_pair[u][:].indirect(offs_sb[:, 16 * a : 16 * a + 16]))
         x_bf = [sb(f"x_bf{a}", [P, S], I32) for a in range(2)]
-        for a in range(2):
-            nc.vector.tensor_copy(
-                x_bf[a][:].rearrange("p (n u) -> p n u", u=2), picked[a][:].bitcast(I32).rearrange("p u n -> p n u")
-            )
+        nc.scalar.copy(
+            x_bf[0][:].bitcast(F32).rearrange("p (n u) -> p n u", u=2),
+            picked[0][:].bitcast(F32).rearrange("p u n -> p n u"),
+        )
+        nc.vector.tensor_copy(
+            x_bf[1][:].rearrange("p (n u) -> p n u", u=2), picked[1][:].bitcast(I32).rearrange("p u n -> p n u")
+        )
         x_code = sb("x_code", [P, S], U32)
         x_scale = sb("x_scale", [P, S], U8)
         for a in range(2):
             cols = slice(a * S // 2, (a + 1) * S // 2)
             nc.vector.quantize_mx(x_code[:, cols].bitcast(FP8X4), x_scale[:, cols], x_bf[a][:].bitcast(BF16))
 
-        w_bf = {key: sb(f"{key[0]}_bf{key[1]}", [P, 2, P, PACK], BF16) for key in (("w1", 0), ("w1", 1), ("w2", 0))}
+        w_bf = {key: sb(f"{key[0]}_bf{key[1]}", [P, 2, P, PACK], BF16) for key in (("w1", 0), ("w1", 1))}
 
-        def deal(copy, name, h, u):
-            src = w_raw[name, h][:].rearrange("p j (m t) -> p m j t", t=PACK)[:, :, :, 2 * u : 2 * u + 2]
-            dst = w_bf[name, u][:].rearrange("p t m j -> p m j t")[:, cuts[name][h] : cuts[name][h + 1]]
-            copy(dst, src)
+        def deal(copy, name, u):
+            src = w_raw[name][:].rearrange("p j (m t) -> p m j t", t=PACK)[:, :, :, 2 * u : 2 * u + 2]
+            copy(w_bf[name, u][:].rearrange("p t m j -> p m j t"), src)
 
         def quantise_w(name, u):
             code = sb(f"{name}_code{u}", [P, H // 2], U32)
@@ -132,25 +129,22 @@ def tile_picked_edgecv_gelu_e_kernel(
                 nc.scalar.copy(row[:, span], acc[:])
             return row
 
-        deal(nc.scalar.copy, "w1", 0, 0)
-        deal(nc.scalar.copy, "w1", 1, 0)
-        deal(nc.scalar.copy, "w1", 0, 1)
+        deal(nc.vector.tensor_copy, "w1", 0)
+        deal(nc.scalar.copy, "w1", 1)
         w1_lo = quantise_w("w1", 0)
-        deal(nc.vector.tensor_copy, "w2", 0, 0)
-        y = [product("y", t, w1_lo, [t]) for t in (0, 1)]
-        deal(nc.vector.tensor_copy, "w1", 1, 1)
-        deal(nc.vector.tensor_copy, "w2", 1, 0)
         w1_hi = quantise_w("w1", 1)
+        y = [product("y", t, w1_lo, [t]) for t in (0, 1)]
+        w_bf["w2", 0] = sb("w2_bf0", [P, 2, P, PACK], BF16, "w1_bf1")
+        deal(nc.vector.tensor_copy, "w2", 0)
         w2_lo = quantise_w("w2", 0)
         e = [product("e", 0, w2_lo, [4, 2]), product("e", 1, w2_lo, [3])]
         w_bf["w2", 1] = sb("w2_bf1", [P, 2, P, PACK], BF16, "w2_code0")
-        deal(nc.scalar.copy, "w2", 0, 1)
-        deal(nc.scalar.copy, "w2", 1, 1)
+        deal(nc.scalar.copy, "w2", 1)
         w2_hi = quantise_w("w2", 1)
         y.extend(product("y", t, w1_hi, [t]) for t in (2, 3))
         e.extend(product("e", t, w2_hi, [t - 2]) for t in (2, 3))
 
-        yc = sb("yc", [P, PACK, V], F32, "w2_bf0")
+        yc = sb("yc", [P, PACK, V], F32, "w1_bf1")
         for t in range(PACK):
             nc.vector.tensor_copy(yc[:, t, :], y[t][:].indirect(cen_sb[:]))
 

@@ -19,7 +19,15 @@ GELU = mybir.ActivationFunctionType.Gelu_apprx_tanh
 
 P = 128
 PACK = 4
-HALF = V // 2
+NEIGHBOURS = 4
+LIST_ROWS = 16
+HALF_S = S // 2
+HALF_T = T // 2
+HALF_V = V // 2
+
+PAIR0_VECTOR = 672
+PAIR1_VECTOR = 336
+DEAL_VECTOR = 48
 
 
 def tile_picked_edgecv_gelu_e_kernel(
@@ -31,52 +39,33 @@ def tile_picked_edgecv_gelu_e_kernel(
         keep = ctx.enter_context(tc.tile_pool(name="keep", bufs=1))
         psum = ctx.enter_context(tc.psum_pool(name="psum", bufs=1))
 
-        def sb(name, shape, dtype, tag=None):
-            return keep.tile(shape, dtype, name=name, tag=tag or name, align_bytes=64)
+        def sb(name, shape, dtype, slot=None):
+            return keep.tile(shape, dtype, name=name, tag=slot or name, align_bytes=64)
 
-        def bank(name, shape, b):
-            return psum.tile(shape, F32, name=name, tag=f"bank{b}")
+        def bank(name, shape, index):
+            return psum.tile(shape, F32, name=name, tag=f"bank{index}")
 
-        warm_in = sb("warm_in", [P, 1], F32)
-        warm_out = sb("warm_out", [P, 1], F32)
-        nc.vector.memset(warm_in[:], 0.0)
-        nc.scalar.activation(warm_out[:], warm_in[:], GELU)
+        def load_list(name, source, entries):
+            tile = lists.tile([P, entries // LIST_ROWS], U16, name=name)
+            nc.sync.dma_start(tile[:], source)
+            return tile
+
         w3_scale = sb("w3_scale", [P, N], U8)
         nc.vector.memset(w3_scale[:].bitcast(I32), 0)
 
         x_rows = xT.rearrange("(p j) n -> p j n", j=PACK)
-        offs_sb = lists.tile([P, S // 16], U16, name="offs_sb")
-        x_pair = [sb(f"x_pair{u}", [P, T], U32) for u in range(2)]
-        x_raw = []
-        pieces = [(0, 0, 1024), (1, 0, 512), (1, 512, 1024)]
-        for n, (u, c0, c1) in enumerate(pieces):
-            x_raw.append(sb(f"x_raw{n}", [P, 2, c1 - c0], F32))
-            nc.sync.dma_start(x_raw[n][:], x_rows[:, 2 * u : 2 * u + 2, c0:c1])
-            if n == 0:
-                nc.sync.dma_start(offs_sb[:], offs)
-
-        def pair_up(copy, n, c0, c1):
-            u, first = pieces[n][:2]
-            copy(
-                x_pair[u][:, c0:c1].bitcast(BF16).rearrange("p (n s) -> p n s", s=2),
-                x_raw[n][:, :, c0 - first : c1 - first].rearrange("p s n -> p n s"),
-            )
-
-        pair_up(nc.vector.tensor_copy, 0, 0, 672)
-        pair_up(nc.scalar.copy, 0, 672, 1024)
-        pair_up(nc.scalar.copy, 1, 0, 512)
-        pair_up(nc.vector.tensor_copy, 2, 512, 848)
-        pair_up(nc.scalar.copy, 2, 848, 1024)
-        w_raw = {}
-        for name, w in (("w1", w1), ("w2", w2)):
-            w_raw[name] = sb(f"{name}_raw", [P, PACK, H], F32)
-            nc.sync.dma_start(w_raw[name][:], w.rearrange("(p j) c -> p j c", j=PACK))
-        cen_sb = lists.tile([P, V // 16], U16, name="cen_sb")
-        nc.sync.dma_start(cen_sb[:], cen)
-        pos_sb = []
-        for d, pos in enumerate((pos1, pos2, pos3, pos4)):
-            pos_sb.append(lists.tile([P, V // 16], U16, name=f"pos_sb{d}"))
-            nc.sync.dma_start(pos_sb[d][:], pos)
+        x_raw0 = sb("x_raw0", [P, 2, T], F32)
+        nc.sync.dma_start(x_raw0[:], x_rows[:, 0:2, :])
+        offs_sb = load_list("offs_sb", offs, S)
+        x_raw1 = [sb(f"x_raw1_{a}", [P, 2, HALF_T], F32) for a in range(2)]
+        for a in range(2):
+            nc.sync.dma_start(x_raw1[a][:], x_rows[:, 2:4, a * HALF_T : (a + 1) * HALF_T])
+        w1_raw = sb("w1_raw", [P, PACK, H], F32)
+        nc.sync.dma_start(w1_raw[:], w1.rearrange("(p j) c -> p j c", j=PACK))
+        w2_raw = sb("w2_raw", [P, PACK, H], F32)
+        nc.sync.dma_start(w2_raw[:], w2.rearrange("(p j) c -> p j c", j=PACK))
+        cen_sb = load_list("cen_sb", cen, V)
+        pos_sb = [load_list(f"pos_sb{d}", pos, V) for d, pos in enumerate((pos1, pos2, pos3, pos4))]
         w3_code = sb("w3_code", [P, 2 * N], U8)
         nc.sync.dma_start(w3_code[:], w3_words[0])
         for q in range(4):
@@ -84,123 +73,130 @@ def tile_picked_edgecv_gelu_e_kernel(
                 w3_scale[32 * q : 32 * q + 4, :].bitcast(I32), w3_scales[0, 4 * q : 4 * q + 4, :].bitcast(I32)
             )
 
-        picked = [sb(f"picked{a}", [P, 2, S // 2], U32) for a in range(2)]
+        x_pair = [sb(f"x_pair{u}", [P, T], U32) for u in range(2)]
+
+        def round_points(copy, u, raw, first_point, c0, c1):
+            words = x_pair[u][:, first_point + c0 : first_point + c1]
+            copy(words.bitcast(BF16).rearrange("p (n s) -> p n s", s=2), raw[:, :, c0:c1].rearrange("p s n -> p n s"))
+
+        round_points(nc.vector.tensor_copy, 0, x_raw0, 0, 0, PAIR0_VECTOR)
+        round_points(nc.scalar.copy, 0, x_raw0, 0, PAIR0_VECTOR, T)
+        round_points(nc.scalar.copy, 1, x_raw1[0], 0, 0, HALF_T)
+        round_points(nc.vector.tensor_copy, 1, x_raw1[1], HALF_T, 0, PAIR1_VECTOR)
+        round_points(nc.scalar.copy, 1, x_raw1[1], HALF_T, PAIR1_VECTOR, HALF_T)
+
+        picked = [sb(f"picked{a}", [P, 2, HALF_S], U32) for a in range(2)]
         for u in range(2):
             for a in range(2):
-                nc.vector.tensor_copy(picked[a][:, u, :], x_pair[u][:].indirect(offs_sb[:, 16 * a : 16 * a + 16]))
-        x_bf = [sb(f"x_bf{a}", [P, S], I32) for a in range(2)]
+                half_list = offs_sb[:, a * HALF_S // LIST_ROWS : (a + 1) * HALF_S // LIST_ROWS]
+                nc.vector.tensor_copy(picked[a][:, u, :], x_pair[u][:].indirect(half_list))
+        x_woven = [sb(f"x_woven{a}", [P, HALF_S * 2], I32) for a in range(2)]
         nc.scalar.copy(
-            x_bf[0][:].bitcast(F32).rearrange("p (n u) -> p n u", u=2),
+            x_woven[0][:].bitcast(F32).rearrange("p (n u) -> p n u", u=2),
             picked[0][:].bitcast(F32).rearrange("p u n -> p n u"),
         )
         nc.vector.tensor_copy(
-            x_bf[1][:].rearrange("p (n u) -> p n u", u=2), picked[1][:].bitcast(I32).rearrange("p u n -> p n u")
+            x_woven[1][:].rearrange("p (n u) -> p n u", u=2), picked[1][:].bitcast(I32).rearrange("p u n -> p n u")
         )
         x_code = sb("x_code", [P, S], U32)
         x_scale = sb("x_scale", [P, S], U8)
         for a in range(2):
-            cols = slice(a * S // 2, (a + 1) * S // 2)
-            nc.vector.quantize_mx(x_code[:, cols].bitcast(FP8X4), x_scale[:, cols], x_bf[a][:].bitcast(BF16))
+            cols = slice(a * HALF_S, (a + 1) * HALF_S)
+            nc.vector.quantize_mx(x_code[:, cols].bitcast(FP8X4), x_scale[:, cols], x_woven[a][:].bitcast(BF16))
 
-        w_bf = {key: sb(f"{key[0]}_bf{key[1]}", [P, 2, P, PACK], BF16) for key in (("w1", 0), ("w1", 1))}
+        def deal(copy, dealt, raw, u, m0, m1):
+            source = raw[:].rearrange("p j (m t) -> p m j t", t=PACK)[:, m0:m1, :, 2 * u : 2 * u + 2]
+            copy(dealt[:].rearrange("p s m j -> p m j s")[:, m0:m1], source)
 
-        def deal(copy, name, u):
-            src = w_raw[name][:].rearrange("p j (m t) -> p m j t", t=PACK)[:, :, :, 2 * u : 2 * u + 2]
-            copy(w_bf[name, u][:].rearrange("p t m j -> p m j t"), src)
-
-        def quantise_w(name, u):
-            code = sb(f"{name}_code{u}", [P, H // 2], U32)
-            scale = sb(f"{name}_scale{u}", [P, H // 2], U8)
-            nc.vector.quantize_mx(code[:].bitcast(FP8X4), scale[:], w_bf[name, u][:].rearrange("p t m j -> p (t m j)"))
+        def quantise_pair(name, dealt):
+            code = sb(f"{name}_code", [P, 2 * P], U32)
+            scale = sb(f"{name}_scale", [P, 2 * P], U8)
+            nc.vector.quantize_mx(code[:].bitcast(FP8X4), scale[:], dealt[:].rearrange("p s m j -> p (s m j)"))
             return code, scale
 
-        def product(name, t, parts, banks):
-            code, scale = parts
-            cols = slice((t % 2) * P, (t % 2 + 1) * P)
-            row = sb(f"{name}_row{t}", [P, S], F32)
-            width = S // len(banks)
-            for n, b in enumerate(banks):
-                acc = bank(f"{name}_acc{t}_{n}", [P, width], b)
-                span = slice(n * width, (n + 1) * width)
-                nc.tensor.matmul_mx(
-                    acc[:], code[:, cols].bitcast(FP8X4), scale[:, cols],
-                    x_code[:, span].bitcast(FP8X4), x_scale[:, span], start=True, stop=True,
-                )
-                nc.scalar.copy(row[:, span], acc[:])
-            return row
-
-        deal(nc.vector.tensor_copy, "w1", 0)
-        deal(nc.scalar.copy, "w1", 1)
-        w1_lo = quantise_w("w1", 0)
-        w1_hi = quantise_w("w1", 1)
-        y = [product("y", t, w1_lo, [t]) for t in (0, 1)]
-        w_bf["w2", 0] = sb("w2_bf0", [P, 2, P, PACK], BF16, "w1_bf1")
-        deal(nc.vector.tensor_copy, "w2", 0)
-        w2_lo = quantise_w("w2", 0)
-        e = [product("e", 0, w2_lo, [4, 2]), product("e", 1, w2_lo, [3])]
-        w_bf["w2", 1] = sb("w2_bf1", [P, 2, P, PACK], BF16, "w2_code0")
-        deal(nc.scalar.copy, "w2", 1)
-        w2_hi = quantise_w("w2", 1)
-        y.extend(product("y", t, w1_hi, [t]) for t in (2, 3))
-        e.extend(product("e", t, w2_hi, [t - 2]) for t in (2, 3))
-
-        yc = sb("yc", [P, PACK, V], F32, "w1_bf1")
-        for t in range(PACK):
-            nc.vector.tensor_copy(yc[:, t, :], y[t][:].indirect(cen_sb[:]))
-
-        g = [sb(f"g{d}", [P, 2, V, 2], BF16) for d in range(4)]
-        for u in range(2):
-            sums = [sb(f"sum{d}_{u}", [P, 2, V], F32, "w2_code0" if (d, u) == (3, 0) else None) for d in range(4)]
+        def products(name, u, weights, first_bank):
+            code, scale = weights
+            rows = []
             for s in range(2):
-                t = 2 * u + s
-                for d in range(4):
-                    nc.vector.tensor_tensor(sums[d][:, s, :], e[t][:].indirect(pos_sb[d][:]), yc[:, t, :], ADD)
-                    if s == 1:
-                        nc.scalar.activation(g[d][:, u], sums[d][:].rearrange("p s v -> p v s"), GELU)
-
-        def larger(name, h, left, right):
-            m = sb(f"{name}_{h}", [P, 2, HALF, 2], BF16)
-            nc.vector.tensor_tensor(m[:], left, right[:, :, h * HALF : (h + 1) * HALF, :], MAX)
-            return m
-
-        m01 = [larger("m01", h, g[0][:, :, h * HALF : (h + 1) * HALF, :], g[1]) for h in range(2)]
-        m012 = [larger("m012", h, m01[h][:], g[2]) for h in range(2)]
-
-        def fourth(h):
-            z = sb(f"z{h}", [P, HALF * PACK], BF16)
-            cols = slice(h * HALF, (h + 1) * HALF)
-            nc.vector.tensor_tensor(
-                z[:].rearrange("p (v u s) -> p v u s", u=2, s=2),
-                m012[h][:].rearrange("p u v s -> p v u s"),
-                g[3][:, :, cols, :].rearrange("p u v s -> p v u s"),
-                MAX,
-            )
-            return z
-
-        out_rows = out.rearrange("(b p) v -> p b v", p=P)
-
-        def project(h, z):
-            z_code = sb(f"z_code{h}", [P, HALF], U32)
-            z_scale = sb(f"z_scale{h}", [P, HALF], U8)
-            nc.vector.quantize_mx(z_code[:].bitcast(FP8X4), z_scale[:], z[:])
-            for b in range(2):
-                acc = bank(f"out_acc{h}_{b}", [P, HALF], 4 + 2 * h + b)
+                acc = bank(f"{name}_acc{2 * u + s}", [P, S], first_bank + s)
+                cols = slice(s * P, (s + 1) * P)
                 nc.tensor.matmul_mx(
-                    acc[:],
-                    w3_code[:, 2 * P * b : 2 * P * (b + 1)].bitcast(FP4X4),
-                    w3_scale[:, P * b : P * (b + 1)],
-                    z_code[:].bitcast(FP8X4),
-                    z_scale[:],
+                    acc[:], code[:, cols].bitcast(FP8X4), scale[:, cols], x_code[:].bitcast(FP8X4), x_scale[:],
                     start=True, stop=True,
                 )
-                res = sb(f"res{h}_{b}", [P, HALF], F32)
-                if h == 1 and b == 1:
-                    nc.vector.tensor_copy(res[:], acc[:])
-                else:
-                    nc.scalar.copy(res[:], acc[:])
-                nc.sync.dma_start(out_rows[:, b, h * HALF : (h + 1) * HALF], res[:])
+                row = sb(f"{name}_row{2 * u + s}", [P, S], F32)
+                nc.scalar.copy(row[:], acc[:])
+                rows.append(row)
+            return rows
 
-        z0 = fourth(0)
-        z1 = fourth(1)
-        project(0, z0)
-        project(1, z1)
+        w1_dealt = [sb(f"w1_dealt{u}", [P, 2, P, PACK], BF16) for u in range(2)]
+        deal(nc.scalar.copy, w1_dealt[0], w1_raw, 0, 0, P)
+        deal(nc.vector.tensor_copy, w1_dealt[1], w1_raw, 1, 0, DEAL_VECTOR)
+        deal(nc.scalar.copy, w1_dealt[1], w1_raw, 1, DEAL_VECTOR, P)
+        y = []
+        for u in range(2):
+            y.extend(products("y", u, quantise_pair(f"w1_{u}", w1_dealt[u]), 2 * u))
+
+        w2_dealt0 = sb("w2_dealt0", [P, 2, P, PACK], BF16, "w1_dealt1")
+        deal(nc.vector.tensor_copy, w2_dealt0, w2_raw, 0, 0, P)
+        e = products("e", 0, quantise_pair("w2_0", w2_dealt0), 4)
+        w2_dealt1 = sb("w2_dealt1", [P, 2, P, PACK], BF16, "w2_0_code")
+        deal(nc.scalar.copy, w2_dealt1, w2_raw, 1, 0, P)
+        e.extend(products("e", 1, quantise_pair("w2_1", w2_dealt1), 6))
+
+        centre = sb("centre", [P, PACK, V], F32, "w1_dealt1")
+        for t in range(PACK):
+            nc.vector.tensor_copy(centre[:, t, :], y[t][:].indirect(cen_sb[:]))
+
+        edge = [sb("edge0", [P, 2, 2, V, 2], BF16), sb("edge1", [P, 2, 2, V, 2], BF16, "w2_1_code")]
+        for u in range(2):
+            sums = [
+                sb(f"sums{u}_0", [P, 2, 2, V], F32),
+                sb(f"sums{u}_1", [P, 2, 2, V], F32, "w2_0_code" if u == 0 else None),
+            ]
+            for s in range(2):
+                t = 2 * u + s
+                for d in range(NEIGHBOURS):
+                    c, b = divmod(d, 2)
+                    nc.vector.tensor_tensor(sums[c][:, b, s, :], e[t][:].indirect(pos_sb[d][:]), centre[:, t, :], ADD)
+                    if s == 1:
+                        nc.scalar.activation(edge[c][:, b, u], sums[c][:, b].rearrange("p s v -> p v s"), GELU)
+
+        def edge_half(d, h):
+            return edge[d // 2][:, d % 2, :, h * HALF_V : (h + 1) * HALF_V, :]
+
+        best = [edge_half(0, h) for h in range(2)]
+        for d in (1, 2):
+            for h in range(2):
+                larger = sb(f"best{d}_{h}", [P, 2, HALF_V, 2], BF16)
+                nc.vector.tensor_tensor(larger[:], best[h], edge_half(d, h), MAX)
+                best[h] = larger[:]
+        z = [sb(f"z{h}", [P, HALF_V * PACK], BF16) for h in range(2)]
+        for h in range(2):
+            nc.vector.tensor_tensor(
+                z[h][:].rearrange("p (v u s) -> p v u s", u=2, s=2),
+                best[h].rearrange("p u v s -> p v u s"),
+                edge_half(3, h).rearrange("p u v s -> p v u s"),
+                MAX,
+            )
+
+        out_rows = out.rearrange("(r p) v -> p r v", p=P)
+        for h in range(2):
+            z_code = sb(f"z_code{h}", [P, HALF_V], U32)
+            z_scale = sb(f"z_scale{h}", [P, HALF_V], U8)
+            nc.vector.quantize_mx(z_code[:].bitcast(FP8X4), z_scale[:], z[h][:])
+            for r in range(N // P):
+                acc = bank(f"out_acc{h}_{r}", [P, HALF_V], 2 * h + r)
+                nc.tensor.matmul_mx(
+                    acc[:],
+                    w3_code[:, 2 * P * r : 2 * P * (r + 1)].bitcast(FP4X4),
+                    w3_scale[:, P * r : P * (r + 1)],
+                    z_code[:].bitcast(FP8X4),
+                    z_scale[:],
+                    start=True,
+                    stop=True,
+                )
+                result = sb(f"result{h}_{r}", [P, HALF_V], F32)
+                copy_out = nc.vector.tensor_copy if (h, r) == (1, 1) else nc.scalar.copy
+                copy_out(result[:], acc[:])
+                nc.sync.dma_start(out_rows[:, r, h * HALF_V : (h + 1) * HALF_V], result[:])

from contextlib import ExitStack

import concourse.mybir as mybir

K, T, S, V, H, N = 512, 1024, 512, 256, 512, 256
FLOPS = 2 * (2 * K * H * S + H * N * V)

F32 = mybir.dt.float32
BF16 = mybir.dt.bfloat16
U32 = mybir.dt.uint32
I32 = mybir.dt.int32
U16 = mybir.dt.uint16
U8 = mybir.dt.uint8
FP8X4 = mybir.dt.float8_e4m3fn_x4
FP4X4 = mybir.dt.float4_e2m1fn_x4
ADD = mybir.AluOpType.add
MAX = mybir.AluOpType.max
GELU = mybir.ActivationFunctionType.Gelu_apprx_tanh

P = 128
PACK = 4
NEIGHBOURS = 4
LIST_ROWS = 16
HALF_S = S // 2
HALF_T = T // 2
HALF_V = V // 2

PAIR0_VECTOR = 672
PAIR1_VECTOR = 336
DEAL_VECTOR = 48


def tile_picked_edgecv_gelu_e_kernel(
    tc, xT, w1, w2, w3_words, w3_scales, offs, cen, pos1, pos2, pos3, pos4, out
):
    nc = tc.nc
    with ExitStack() as ctx:
        lists = ctx.enter_context(tc.tile_pool(name="lists", bufs=1))
        keep = ctx.enter_context(tc.tile_pool(name="keep", bufs=1))
        psum = ctx.enter_context(tc.psum_pool(name="psum", bufs=1))

        def sb(name, shape, dtype, slot=None):
            return keep.tile(shape, dtype, name=name, tag=slot or name, align_bytes=64)

        def bank(name, shape, index):
            return psum.tile(shape, F32, name=name, tag=f"bank{index}")

        def load_list(name, source, entries):
            tile = lists.tile([P, entries // LIST_ROWS], U16, name=name)
            nc.sync.dma_start(tile[:], source)
            return tile

        w3_scale = sb("w3_scale", [P, N], U8)
        nc.vector.memset(w3_scale[:].bitcast(I32), 0)

        x_rows = xT.rearrange("(p j) n -> p j n", j=PACK)
        x_raw0 = sb("x_raw0", [P, 2, T], F32)
        nc.sync.dma_start(x_raw0[:], x_rows[:, 0:2, :])
        offs_sb = load_list("offs_sb", offs, S)
        x_raw1 = [sb(f"x_raw1_{a}", [P, 2, HALF_T], F32) for a in range(2)]
        for a in range(2):
            nc.sync.dma_start(x_raw1[a][:], x_rows[:, 2:4, a * HALF_T : (a + 1) * HALF_T])
        w1_raw = sb("w1_raw", [P, PACK, H], F32)
        nc.sync.dma_start(w1_raw[:], w1.rearrange("(p j) c -> p j c", j=PACK))
        w2_raw = sb("w2_raw", [P, PACK, H], F32)
        nc.sync.dma_start(w2_raw[:], w2.rearrange("(p j) c -> p j c", j=PACK))
        cen_sb = load_list("cen_sb", cen, V)
        pos_sb = [load_list(f"pos_sb{d}", pos, V) for d, pos in enumerate((pos1, pos2, pos3, pos4))]
        w3_code = sb("w3_code", [P, 2 * N], U8)
        nc.sync.dma_start(w3_code[:], w3_words[0])
        for q in range(4):
            nc.sync.dma_start(
                w3_scale[32 * q : 32 * q + 4, :].bitcast(I32), w3_scales[0, 4 * q : 4 * q + 4, :].bitcast(I32)
            )

        x_pair = [sb(f"x_pair{u}", [P, T], U32) for u in range(2)]

        def round_points(copy, u, raw, first_point, c0, c1):
            words = x_pair[u][:, first_point + c0 : first_point + c1]
            copy(words.bitcast(BF16).rearrange("p (n s) -> p n s", s=2), raw[:, :, c0:c1].rearrange("p s n -> p n s"))

        round_points(nc.vector.tensor_copy, 0, x_raw0, 0, 0, PAIR0_VECTOR)
        round_points(nc.scalar.copy, 0, x_raw0, 0, PAIR0_VECTOR, T)
        round_points(nc.scalar.copy, 1, x_raw1[0], 0, 0, HALF_T)
        round_points(nc.vector.tensor_copy, 1, x_raw1[1], HALF_T, 0, PAIR1_VECTOR)
        round_points(nc.scalar.copy, 1, x_raw1[1], HALF_T, PAIR1_VECTOR, HALF_T)

        picked = [sb(f"picked{a}", [P, 2, HALF_S], U32) for a in range(2)]
        for u in range(2):
            for a in range(2):
                half_list = offs_sb[:, a * HALF_S // LIST_ROWS : (a + 1) * HALF_S // LIST_ROWS]
                nc.vector.tensor_copy(picked[a][:, u, :], x_pair[u][:].indirect(half_list))
        x_woven = [sb(f"x_woven{a}", [P, HALF_S * 2], I32) for a in range(2)]
        nc.scalar.copy(
            x_woven[0][:].bitcast(F32).rearrange("p (n u) -> p n u", u=2),
            picked[0][:].bitcast(F32).rearrange("p u n -> p n u"),
        )
        nc.vector.tensor_copy(
            x_woven[1][:].rearrange("p (n u) -> p n u", u=2), picked[1][:].bitcast(I32).rearrange("p u n -> p n u")
        )
        x_code = sb("x_code", [P, S], U32)
        x_scale = sb("x_scale", [P, S], U8)
        for a in range(2):
            cols = slice(a * HALF_S, (a + 1) * HALF_S)
            nc.vector.quantize_mx(x_code[:, cols].bitcast(FP8X4), x_scale[:, cols], x_woven[a][:].bitcast(BF16))

        def deal(copy, dealt, raw, u, m0, m1):
            source = raw[:].rearrange("p j (m t) -> p m j t", t=PACK)[:, m0:m1, :, 2 * u : 2 * u + 2]
            copy(dealt[:].rearrange("p s m j -> p m j s")[:, m0:m1], source)

        def quantise_pair(name, dealt):
            code = sb(f"{name}_code", [P, 2 * P], U32)
            scale = sb(f"{name}_scale", [P, 2 * P], U8)
            nc.vector.quantize_mx(code[:].bitcast(FP8X4), scale[:], dealt[:].rearrange("p s m j -> p (s m j)"))
            return code, scale

        def products(name, u, weights, first_bank):
            code, scale = weights
            rows = []
            for s in range(2):
                acc = bank(f"{name}_acc{2 * u + s}", [P, S], first_bank + s)
                cols = slice(s * P, (s + 1) * P)
                nc.tensor.matmul_mx(
                    acc[:], code[:, cols].bitcast(FP8X4), scale[:, cols], x_code[:].bitcast(FP8X4), x_scale[:],
                    start=True, stop=True,
                )
                row = sb(f"{name}_row{2 * u + s}", [P, S], F32)
                nc.scalar.copy(row[:], acc[:])
                rows.append(row)
            return rows

        w1_dealt = [sb(f"w1_dealt{u}", [P, 2, P, PACK], BF16) for u in range(2)]
        deal(nc.scalar.copy, w1_dealt[0], w1_raw, 0, 0, P)
        deal(nc.vector.tensor_copy, w1_dealt[1], w1_raw, 1, 0, DEAL_VECTOR)
        deal(nc.scalar.copy, w1_dealt[1], w1_raw, 1, DEAL_VECTOR, P)
        y = []
        for u in range(2):
            y.extend(products("y", u, quantise_pair(f"w1_{u}", w1_dealt[u]), 2 * u))

        w2_dealt0 = sb("w2_dealt0", [P, 2, P, PACK], BF16, "w1_dealt1")
        deal(nc.vector.tensor_copy, w2_dealt0, w2_raw, 0, 0, P)
        e = products("e", 0, quantise_pair("w2_0", w2_dealt0), 4)
        w2_dealt1 = sb("w2_dealt1", [P, 2, P, PACK], BF16, "w2_0_code")
        deal(nc.scalar.copy, w2_dealt1, w2_raw, 1, 0, P)
        e.extend(products("e", 1, quantise_pair("w2_1", w2_dealt1), 6))

        centre = sb("centre", [P, PACK, V], F32, "w1_dealt1")
        for t in range(PACK):
            nc.vector.tensor_copy(centre[:, t, :], y[t][:].indirect(cen_sb[:]))

        edge = [sb("edge0", [P, 2, 2, V, 2], BF16), sb("edge1", [P, 2, 2, V, 2], BF16, "w2_1_code")]
        for u in range(2):
            sums = [
                sb(f"sums{u}_0", [P, 2, 2, V], F32),
                sb(f"sums{u}_1", [P, 2, 2, V], F32, "w2_0_code" if u == 0 else None),
            ]
            for s in range(2):
                t = 2 * u + s
                for d in range(NEIGHBOURS):
                    c, b = divmod(d, 2)
                    nc.vector.tensor_tensor(sums[c][:, b, s, :], e[t][:].indirect(pos_sb[d][:]), centre[:, t, :], ADD)
                    if s == 1:
                        nc.scalar.activation(edge[c][:, b, u], sums[c][:, b].rearrange("p s v -> p v s"), GELU)

        def edge_half(d, h):
            return edge[d // 2][:, d % 2, :, h * HALF_V : (h + 1) * HALF_V, :]

        best = [edge_half(0, h) for h in range(2)]
        for d in (1, 2):
            for h in range(2):
                larger = sb(f"best{d}_{h}", [P, 2, HALF_V, 2], BF16)
                nc.vector.tensor_tensor(larger[:], best[h], edge_half(d, h), MAX)
                best[h] = larger[:]
        z = [sb(f"z{h}", [P, HALF_V * PACK], BF16) for h in range(2)]
        for h in range(2):
            nc.vector.tensor_tensor(
                z[h][:].rearrange("p (v u s) -> p v u s", u=2, s=2),
                best[h].rearrange("p u v s -> p v u s"),
                edge_half(3, h).rearrange("p u v s -> p v u s"),
                MAX,
            )

        out_rows = out.rearrange("(r p) v -> p r v", p=P)
        for h in range(2):
            z_code = sb(f"z_code{h}", [P, HALF_V], U32)
            z_scale = sb(f"z_scale{h}", [P, HALF_V], U8)
            nc.vector.quantize_mx(z_code[:].bitcast(FP8X4), z_scale[:], z[h][:])
            for r in range(N // P):
                acc = bank(f"out_acc{h}_{r}", [P, HALF_V], 2 * h + r)
                nc.tensor.matmul_mx(
                    acc[:],
                    w3_code[:, 2 * P * r : 2 * P * (r + 1)].bitcast(FP4X4),
                    w3_scale[:, P * r : P * (r + 1)],
                    z_code[:].bitcast(FP8X4),
                    z_scale[:],
                    start=True,
                    stop=True,
                )
                result = sb(f"result{h}_{r}", [P, HALF_V], F32)
                copy_out = nc.vector.tensor_copy if (h, r) == (1, 1) else nc.scalar.copy
                copy_out(result[:], acc[:])
                nc.sync.dma_start(out_rows[:, r, h * HALF_V : (h + 1) * HALF_V], result[:])
